import numpy as np
import ml_dtypes


def mxq(x, axis, fmt="e4m3"):
    dtype, down = {"e4m3": (ml_dtypes.float8_e4m3fn, 7), "e5m2": (ml_dtypes.float8_e5m2, 14)}[fmt]
    v = np.moveaxis(np.asarray(x, np.float32).astype(ml_dtypes.bfloat16).astype(np.float64), axis, -1)
    blocks = v.reshape(v.shape[:-1] + (-1, 32))
    amax = np.abs(blocks).max(-1, keepdims=True)
    byte = np.maximum(np.where(amax > 0, np.frexp(amax)[1] - 1 + 127, 0) - down, 1)
    scale = np.exp2(byte - 127.0)
    codes = (blocks / scale).astype(np.float32).astype(dtype).astype(np.float64)
    return np.moveaxis((codes * scale).reshape(v.shape), -1, axis)


WIDE = False


def mx_kscale(k):
    if not WIDE:
        return np.ones(k)
    levels = np.array([10, -10, 5, -5, 0])
    if k % 512:
        return np.exp2(np.random.permutation(np.resize(levels, k // 32))).repeat(32)
    a = np.empty((k // 512, 16))
    for p in range(k // 512):
        a[p, :8] = np.random.permutation(np.resize(levels, 8))
        for g in range(8):
            far = levels[np.abs(levels - a[p, g]) >= 10]
            a[p, g + 8] = far[np.random.randint(len(far))]
    return np.exp2(a.ravel()).repeat(32)


def f64(x):
    return np.asarray(x).astype(np.float64)


def striped(idx):
    return np.tile(idx.reshape(-1, 16).T, (8, 1)).astype(np.uint16)


def unstriped(offs):
    return offs[:16].T.reshape(-1).astype(np.int64)


def striped8(idx):
    return np.concatenate([x.reshape(-1, 16).T for x in idx]).astype(np.uint16)


def runs(offs, k):
    lists = np.stack([offs[16 * r : 16 * r + 16].T.reshape(-1) for r in range(8)]).astype(np.int64)
    return lists[np.arange(k) % 512 // 64]


def pack_weight(w):
    k, n = w.shape
    w = f64(np.asarray(w, np.float32).astype(ml_dtypes.bfloat16)).reshape(k // 32, 32, n)
    amax = np.abs(w).max(1)
    byte = np.clip(np.where(amax > 0, np.frexp(amax)[1] - 1 + 127 - 7, 1), 1, 254)
    scaled = (w * np.exp2(127.0 - byte)[:, None, :]).reshape(k, n).astype(np.float32)
    words = np.ascontiguousarray(scaled.reshape(k // 512, 128, 4, n).transpose(0, 1, 3, 2)).astype(ml_dtypes.float8_e4m3fn).view(np.uint8)
    return words, np.ascontiguousarray(byte.astype(np.uint8).reshape(k // 512, 16, n))


def unpack_weight(words, scales):
    g, p, n, _ = words.shape
    vals = np.ascontiguousarray(words).view(ml_dtypes.float8_e4m3fn).astype(np.float64) * np.repeat(np.exp2(scales.astype(np.float64) - 127.0), 8, axis=1)[..., None]
    return vals.transpose(0, 1, 3, 2).reshape(g * 512, n)


def sigmoid(v):
    return 1.0 / (1.0 + np.exp(-np.maximum(v, -700.0)))


K, T, S, H = 512, 2048, 512, 512


def setup_inputs():
    n = np.random.standard_normal
    s = mx_kscale(K)[:, None]
    u = mx_kscale(S)
    packed_xT = pack_weight(n((K, T)) * s)
    return {
        "x_words": packed_xT[0],
        "x_scales": packed_xT[1],
        "wa": (n((K, H)) / np.sqrt(K) / s).astype(np.float32),
        "wb": (n((K, H)) / np.sqrt(K) / s).astype(np.float32),
        "gt": (np.random.uniform(0.5, 1.5, (S, 1)) * u[:, None]).astype(np.float32),
        "gi": (np.random.uniform(0.5, 1.5, (S, 1)) / u[:, None]).astype(np.float32),
        "offs": striped(np.random.permutation(T)[:S]),
        "two": striped(np.random.permutation(T)[:S]),
        "n1": striped8(np.stack([np.random.permutation(H) for _ in range(8)])),
        "n2": striped8(np.stack([np.random.permutation(H) for _ in range(8)])),
        "n3": striped8(np.stack([np.random.permutation(H) for _ in range(8)])),
        "n4": striped8(np.stack([np.random.permutation(H) for _ in range(8)])),
        "n5": striped8(np.stack([np.random.permutation(H) for _ in range(8)])),
    }


def reference(x_words, x_scales, wa, wb, gt, gi, offs, two, n1, n2, n3, n4, n5):
    xq = unpack_weight(x_words, x_scales)[:, unstriped(offs)]
    a = xq.T @ mxq(f64(wa), 0, "e4m3")
    x_two = unpack_weight(x_words, x_scales)[:, unstriped(two)]
    b = x_two.T @ mxq(f64(wb), 0, "e4m3")
    z = f64(gt) * (np.maximum(a[np.arange(S)[:, None], runs(n1, S)] + b[np.arange(S)[:, None], runs(n3, S)], a[np.arange(S)[:, None], runs(n2, S)] + b[np.arange(S)[:, None], runs(n4, S)]))
    z2 = f64(gi) * b
    cv = 0.0625 * ((mxq(z, 0, "e4m3").T @ mxq(z2, 0, "e4m3")))
    return cv * (sigmoid(cv[np.arange(H)[:, None], runs(n5, H)]))

@@ -1,0 +1,172 @@
+from contextlib import ExitStack
+
+import concourse.mybir as mybir
+
+K, T, S, H = 512, 2048, 512, 512
+FLOPS = 3 * 2 * 512 * 512 * 512
+
+F32 = mybir.dt.float32
+BF16 = mybir.dt.bfloat16
+I32 = mybir.dt.int32
+U32 = mybir.dt.uint32
+U16 = mybir.dt.uint16
+U8 = mybir.dt.uint8
+FP8X4 = mybir.dt.float8_e4m3fn_x4
+ALU = mybir.AluOpType
+ACT = mybir.ActivationFunctionType
+
+P = 128
+PACK = 4
+HALF = H // 2
+LIST_COLS = S // 16
+
+
+def tile_picked_momtpathbgate_none_p_kernel(tc, x_words, x_scales, wa, wb, gt, gi, offs, two, n1, n2, n3, n4, n5, out):
+    nc = tc.nc
+    with ExitStack() as ctx:
+        keep = ctx.enter_context(tc.tile_pool(name="keep", bufs=1))
+        psum = ctx.enter_context(tc.psum_pool(name="psum", bufs=1))
+
+        def load_list(name, src):
+            lst = keep.tile([P, LIST_COLS], U16, name=name)
+            nc.sync.dma_start(lst[:], src)
+            return lst
+
+        def load_weight(name, w, cols):
+            raw = keep.tile([P, PACK, cols.stop - cols.start], F32, name=name)
+            nc.sync.dma_start(raw[:], w.rearrange("(p j) n -> p j n", j=PACK)[:, :, cols])
+            return raw
+
+        halves = [slice(h * HALF, (h + 1) * HALF) for h in range(2)]
+        scale_rows = keep.tile([P, T // 4], I32, name="scale_rows", align_bytes=64)
+        scale_table = keep.tile([P, T], U8, name="scale_table", align_bytes=64)
+        word_table = keep.tile([P, T], I32, name="word_table", align_bytes=64)
+        nc.vector.memset(scale_table[:].bitcast(I32), 0)
+
+        for q in range(4):
+            nc.sync.dma_start(scale_rows[32 * q:32 * q + 4, :], x_scales[0, 4 * q:4 * q + 4, :].bitcast(I32))
+        two_l = load_list("two_l", two)
+        offs_l = load_list("offs_l", offs)
+        wb_whole = load_weight("wb_raw", wb, slice(0, H))
+        wb_raw = [wb_whole[:, :, cols] for cols in halves]
+        nc.sync.dma_start(word_table[:], x_words[0].rearrange("p c r -> p (c r)").bitcast(I32))
+        gt_t = keep.tile([P, PACK], F32, name="gt_t")
+        gi_t = keep.tile([P, PACK], F32, name="gi_t")
+        nc.sync.dma_start(gt_t[:], gt.rearrange("(p t) o -> p (t o)", t=PACK))
+        nc.sync.dma_start(gi_t[:], gi.rearrange("(p t) o -> p (t o)", t=PACK))
+        n3_l = load_list("n3_l", n3)
+        n4_l = load_list("n4_l", n4)
+        wa_raw = [load_weight("wa_raw%d" % h, wa, halves[h])[:] for h in range(2)]
+        n1_l = load_list("n1_l", n1)
+        n2_l = load_list("n2_l", n2)
+        n5_l = load_list("n5_l", n5)
+        for q in range(4):
+            nc.vector.tensor_copy(scale_table[32 * q:32 * q + 4, :].bitcast(I32), scale_rows[32 * q:32 * q + 4, :])
+
+        gt_sign = keep.tile([P, PACK], F32, name="gt_sign")
+        gt_step = keep.tile([P, PACK], F32, name="gt_step")
+        gi_signed = keep.tile([P, PACK], F32, name="gi_signed")
+        nc.gpsimd.tensor_scalar(gt_step[:], gt_t[:], 0.0, 2.0, ALU.is_ge, ALU.mult)
+        nc.gpsimd.tensor_scalar(gt_sign[:], gt_step[:], 1.0, -1.0, ALU.mult, ALU.add)
+        nc.gpsimd.tensor_tensor(gi_signed[:], gi_t[:], gt_sign[:], ALU.mult)
+
+        def pick_scales(name, lst):
+            picked = keep.tile([P, S], U8, name=name + "_picked", align_bytes=64)
+            dealt = keep.tile([P, PACK, P], U8, name=name + "_dealt", align_bytes=64)
+            nc.vector.tensor_copy(picked[:], scale_table[:].indirect(lst[:]))
+            nc.vector.tensor_copy(dealt[:], picked[:].rearrange("p (m t) -> p t m", t=PACK))
+            return dealt
+
+        def pick_words(name, lst):
+            dealt = keep.tile([P, PACK, P], U32, name=name, align_bytes=64)
+            nc.vector.tensor_copy(dealt[:].rearrange("p t m -> p m t"), word_table[:].bitcast(U32).indirect(lst[:]))
+            return dealt
+
+        def interleave(copy, dst, src):
+            copy(dst.rearrange("p (c i) t -> p c t i", i=4), src.rearrange("p t (c i) -> p c t i", i=4))
+
+        def quantize(codes, scales, grouped):
+            nc.vector.quantize_mx(out=codes.bitcast(FP8X4), scales=scales, in_=grouped)
+
+        def quantize_weight(name, raws, copies):
+            codes = keep.tile([P, H], U32, name=name + "_codes", align_bytes=64)
+            scales = keep.tile([P, H], U8, name=name + "_scales", align_bytes=64)
+            grouped = keep.tile([P, H, PACK], BF16, name=name + "_grouped", align_bytes=64)
+            for h in range(2):
+                interleave(copies[h], grouped[:, halves[h], :], raws[h])
+            for cols in halves:
+                quantize(codes[:, cols], scales[:, cols], grouped[:, cols, :].rearrange("p c t -> p (c t)"))
+            return codes, scales
+
+        def product(bank, lhs_codes, lhs_scales, rhs_codes, rhs_scales):
+            nc.tensor.matmul_mx(out=bank, lhsT=lhs_codes.bitcast(FP8X4), lhsT_scale=lhs_scales,
+                                rhs=rhs_codes.bitcast(FP8X4), rhs_scale=rhs_scales, start=True, stop=True)
+
+        xb_scales = pick_scales("xb_scales", two_l)
+        xa_scales = pick_scales("xa_scales", offs_l)
+        wb_codes, wb_scales = quantize_weight("wb", wb_raw, [nc.scalar.copy, nc.scalar.copy])
+        xb_words = pick_words("xb_words", two_l)
+        xa_words = pick_words("xa_words", offs_l)
+        wa_codes, wa_scales = quantize_weight("wa", wa_raw, [nc.scalar.copy, nc.vector.tensor_copy])
+        gt_abs = keep.tile([P, PACK], F32, name="gt_abs", tag="wa_raw0")
+        nc.scalar.activation(gt_abs[:], gt_t[:], ACT.Abs)
+
+        b_banks, a_banks = [], []
+        for t in range(PACK):
+            bank = psum.tile([P, H], F32, name="b_bank%d" % t, tag="left%d" % t)
+            product(bank[:], xb_words[:, t, :], xb_scales[:, t, :], wb_codes[:], wb_scales[:])
+            b_banks.append(bank)
+        for t in range(PACK):
+            bank = psum.tile([P, H], F32, name="a_bank%d" % t, tag="right%d" % t)
+            product(bank[:], xa_words[:, t, :], xa_scales[:, t, :], wa_codes[:], wa_scales[:])
+            a_banks.append(bank)
+        a_rows = [keep.tile([P, H], F32, name="a_rows%d" % t) for t in range(PACK)]
+        b_rows = [keep.tile([P, H], F32, name="b_rows%d" % t, align_bytes=64) for t in range(PACK)]
+
+        z_grouped = keep.tile([P, PACK, P, PACK], BF16, name="z_grouped", align_bytes=64)
+        for h in range(2):
+            part = slice(h * LIST_COLS // 2, (h + 1) * LIST_COLS // 2)
+            totals = [keep.tile([P, PACK, HALF], F32, name="sum%d_%d" % (h, k)) for k in range(2)]
+            for t in range(PACK):
+                if h == 0:
+                    nc.scalar.activation(b_rows[t][:], b_banks[t][:], ACT.Copy, scale=gt_abs[:, t:t + 1])
+                    if t < 3:
+                        nc.vector.tensor_scalar(a_rows[t][:], a_banks[t][:], gt_abs[:, t:t + 1], None, ALU.mult)
+                    else:
+                        nc.scalar.activation(a_rows[t][:], a_banks[t][:], ACT.Copy, scale=gt_abs[:, t:t + 1])
+                for k, (a_list, b_list) in enumerate(((n1_l, n3_l), (n2_l, n4_l))):
+                    from_b = keep.tile([P, HALF], F32, name="from_b%d_%d" % (k, t))
+                    nc.scalar.activation(from_b[:], b_rows[t][:].indirect(b_list[:, part]), ACT.Copy)
+                    nc.vector.tensor_tensor(totals[k][:, t, :], a_rows[t][:].indirect(a_list[:, part]), from_b[:], ALU.add)
+            sums = [total[:].rearrange("p t (m u) -> p m t u", u=PACK) for total in totals]
+            ms = slice(h * P // 2, (h + 1) * P // 2)
+            nc.vector.tensor_tensor(z_grouped[:, :, ms, :].rearrange("p u m t -> p m t u"), sums[0], sums[1], ALU.max)
+
+        z2_grouped = keep.tile([P, H, PACK], BF16, name="z2_grouped", align_bytes=64)
+        z2_codes = keep.tile([P, H], U32, name="z2_codes", tag="wa_codes", align_bytes=64)
+        z2_scales = keep.tile([P, H], U8, name="z2_scales", tag="wa_scales", align_bytes=64)
+        z2_planes = keep.tile([P, PACK, H], BF16, name="z2_planes", tag="b_rows3", align_bytes=64)
+        for t in range(PACK):
+            nc.scalar.activation(z2_planes[:, t, :], b_banks[t][:], ACT.Copy, scale=gi_signed[:, t:t + 1])
+        for cols, copy in zip(halves, (nc.scalar.copy, nc.vector.tensor_copy)):
+            interleave(copy, z2_grouped[:, cols, :], z2_planes[:, :, cols])
+
+        out_rows = out.rearrange("(m u) n -> u m n", u=PACK)
+        for u in range(PACK):
+            z_codes = keep.tile([P, P], U32, name="z_codes%d" % u, align_bytes=64)
+            z_scales = keep.tile([P, P], U8, name="z_scales%d" % u, align_bytes=64)
+            quantize(z_codes[:], z_scales[:], z_grouped[:, u, :, :].rearrange("p m t -> p (m t)"))
+            if u == 0:
+                quantize(z2_codes[:], z2_scales[:], z2_grouped[:].rearrange("p c t -> p (c t)"))
+            bank = psum.tile([P, H], F32, name="cv_bank%d" % u, tag="right%d" % u)
+            product(bank[:], z_codes[:], z_scales[:], z2_codes[:], z2_scales[:])
+            cv = keep.tile([P, H], F32, name="cv%d" % u)
+            nc.vector.tensor_scalar(cv[:], bank[:], 0.0625, None, ALU.mult)
+            gate = keep.tile([P, H], F32, name="gate%d" % u)
+            result = keep.tile([P, H], F32, name="result%d" % u)
+            for h in range(2):
+                part = slice(h * LIST_COLS // 2, (h + 1) * LIST_COLS // 2)
+                nc.scalar.activation(gate[:, halves[h]], cv[:].indirect(n5_l[:, part]), ACT.Sigmoid)
+            for cols in (halves if u == PACK - 1 else [slice(0, H)]):
+                nc.vector.tensor_tensor(result[:, cols], cv[:, cols], gate[:, cols], ALU.mult)
+                nc.sync.dma_start(out_rows[u][:, cols], result[:, cols])

@@ -1,6 +1,7 @@
 from contextlib import ExitStack
 
 import concourse.mybir as mybir
+from concourse.masks import make_identity
 
 K, T, S, H = 512, 2048, 512, 512
 FLOPS = 3 * 2 * 512 * 512 * 512
@@ -47,13 +48,17 @@ def tile_picked_momtpathbgate_none_p_kernel(tc, x_words, x_scales, wa, wb, gt, g
             nc.sync.dma_start(scale_rows[32 * q:32 * q + 4, :], x_scales[0, 4 * q:4 * q + 4, :].bitcast(I32))
         two_l = load_list("two_l", two)
         offs_l = load_list("offs_l", offs)
-        wb_whole = load_weight("wb_raw", wb, slice(0, H))
-        wb_raw = [wb_whole[:, :, cols] for cols in halves]
         nc.sync.dma_start(word_table[:], x_words[0].rearrange("p c r -> p (c r)").bitcast(I32))
-        gt_t = keep.tile([P, PACK], F32, name="gt_t")
-        gi_t = keep.tile([P, PACK], F32, name="gi_t")
-        nc.sync.dma_start(gt_t[:], gt.rearrange("(p t) o -> p (t o)", t=PACK))
-        nc.sync.dma_start(gi_t[:], gi.rearrange("(p t) o -> p (t o)", t=PACK))
+        wb_raw = [load_weight("wb_raw%d" % h, wb, halves[h])[:] for h in range(2)]
+        gains_by_tile = keep.tile([P, P], F32, name="gains_by_tile")
+        identity = keep.tile([P, P], F32, name="identity")
+        nc.gpsimd.memset(gains_by_tile[:], 0.0)
+        make_identity(nc, identity[:])
+        unread = keep.tile([P, 1], F32, name="unread")
+        nc.scalar.activation(unread[:], identity[:, 0:1], ACT.Sigmoid)
+        for n, gain in enumerate((gt, gi)):
+            nc.sync.dma_start(gains_by_tile[PACK * n:PACK * (n + 1), :].rearrange("t (g i) -> t g i", i=4),
+                              gain.rearrange("(g t i) o -> t g (i o)", t=PACK, i=4))
         n3_l = load_list("n3_l", n3)
         n4_l = load_list("n4_l", n4)
         wa_raw = [load_weight("wa_raw%d" % h, wa, halves[h])[:] for h in range(2)]
@@ -63,23 +68,29 @@ def tile_picked_momtpathbgate_none_p_kernel(tc, x_words, x_scales, wa, wb, gt, g
         for q in range(4):
             nc.vector.tensor_copy(scale_table[32 * q:32 * q + 4, :].bitcast(I32), scale_rows[32 * q:32 * q + 4, :])
 
+        gains_bank = psum.tile([P, P], F32, name="gains_bank", tag="right3")
+        nc.tensor.transpose(gains_bank[:], gains_by_tile[:], identity[:])
+        gains = keep.tile([P, 2 * PACK], F32, name="gains")
+        nc.scalar.copy(gains[:], gains_bank[:, 0:2 * PACK])
+        gt_t, gi_t = gains[:, 0:PACK], gains[:, PACK:2 * PACK]
         gt_sign = keep.tile([P, PACK], F32, name="gt_sign")
         gt_step = keep.tile([P, PACK], F32, name="gt_step")
         gi_signed = keep.tile([P, PACK], F32, name="gi_signed")
-        nc.gpsimd.tensor_scalar(gt_step[:], gt_t[:], 0.0, 2.0, ALU.is_ge, ALU.mult)
+        nc.gpsimd.tensor_scalar(gt_step[:], gt_t, 0.0, 2.0, ALU.is_ge, ALU.mult)
         nc.gpsimd.tensor_scalar(gt_sign[:], gt_step[:], 1.0, -1.0, ALU.mult, ALU.add)
-        nc.gpsimd.tensor_tensor(gi_signed[:], gi_t[:], gt_sign[:], ALU.mult)
+        nc.gpsimd.tensor_tensor(gi_signed[:], gi_t, gt_sign[:], ALU.mult)
 
         def pick_scales(name, lst):
             picked = keep.tile([P, S], U8, name=name + "_picked", align_bytes=64)
-            dealt = keep.tile([P, PACK, P], U8, name=name + "_dealt", align_bytes=64)
+            dealt = keep.tile([P, S], U8, name=name + "_dealt", align_bytes=64)
             nc.vector.tensor_copy(picked[:], scale_table[:].indirect(lst[:]))
-            nc.vector.tensor_copy(dealt[:], picked[:].rearrange("p (m t) -> p t m", t=PACK))
-            return dealt
+            nc.vector.tensor_copy(dealt[:].bitcast(I32).rearrange("p (t g) -> p t g", t=PACK),
+                                  picked[:].bitcast(I32).rearrange("p (g t) -> p t g", t=PACK))
+            return dealt[:].rearrange("p (t m) -> p t m", t=PACK)
 
         def pick_words(name, lst):
             dealt = keep.tile([P, PACK, P], U32, name=name, align_bytes=64)
-            nc.vector.tensor_copy(dealt[:].rearrange("p t m -> p m t"), word_table[:].bitcast(U32).indirect(lst[:]))
+            nc.vector.tensor_copy(dealt[:].rearrange("p t (g i) -> p g t i", i=4), word_table[:].bitcast(U32).indirect(lst[:]))
             return dealt
 
         def interleave(copy, dst, src):
@@ -103,27 +114,33 @@ def tile_picked_momtpathbgate_none_p_kernel(tc, x_words, x_scales, wa, wb, gt, g
                                 rhs=rhs_codes.bitcast(FP8X4), rhs_scale=rhs_scales, start=True, stop=True)
 
         xb_scales = pick_scales("xb_scales", two_l)
-        xa_scales = pick_scales("xa_scales", offs_l)
-        wb_codes, wb_scales = quantize_weight("wb", wb_raw, [nc.scalar.copy, nc.scalar.copy])
         xb_words = pick_words("xb_words", two_l)
+        wb_codes, wb_scales = quantize_weight("wb", wb_raw, [nc.scalar.copy, nc.scalar.copy])
+        xa_scales = pick_scales("xa_scales", offs_l)
         xa_words = pick_words("xa_words", offs_l)
         wa_codes, wa_scales = quantize_weight("wa", wa_raw, [nc.scalar.copy, nc.vector.tensor_copy])
         gt_abs = keep.tile([P, PACK], F32, name="gt_abs", tag="wa_raw0")
-        nc.scalar.activation(gt_abs[:], gt_t[:], ACT.Abs)
+        nc.scalar.activation(gt_abs[:], gt_t, ACT.Abs)
 
         b_banks, a_banks = [], []
         for t in range(PACK):
             bank = psum.tile([P, H], F32, name="b_bank%d" % t, tag="left%d" % t)
             product(bank[:], xb_words[:, t, :], xb_scales[:, t, :], wb_codes[:], wb_scales[:])
             b_banks.append(bank)
-        for t in range(PACK):
             bank = psum.tile([P, H], F32, name="a_bank%d" % t, tag="right%d" % t)
             product(bank[:], xa_words[:, t, :], xa_scales[:, t, :], wa_codes[:], wa_scales[:])
             a_banks.append(bank)
         a_rows = [keep.tile([P, H], F32, name="a_rows%d" % t) for t in range(PACK)]
         b_rows = [keep.tile([P, H], F32, name="b_rows%d" % t, align_bytes=64) for t in range(PACK)]
 
-        z_grouped = keep.tile([P, PACK, P, PACK], BF16, name="z_grouped", align_bytes=64)
+        z_grouped = [keep.tile([P, P, PACK], BF16, name="z_grouped%d" % u, align_bytes=64) for u in range(PACK)]
+        sums = []
+
+        def larger(h, u):
+            first, second = [total[:].rearrange("p t (g u i) -> p u g t i", u=PACK, i=4)[:, u] for total in sums[h]]
+            dst = z_grouped[u][:, h * P // 2:(h + 1) * P // 2, :].rearrange("p (g i) t -> p g t i", i=4)
+            nc.vector.tensor_tensor(dst, first, second, ALU.max)
+
         for h in range(2):
             part = slice(h * LIST_COLS // 2, (h + 1) * LIST_COLS // 2)
             totals = [keep.tile([P, PACK, HALF], F32, name="sum%d_%d" % (h, k)) for k in range(2)]
@@ -138,9 +155,10 @@ def tile_picked_momtpathbgate_none_p_kernel(tc, x_words, x_scales, wa, wb, gt, g
                     from_b = keep.tile([P, HALF], F32, name="from_b%d_%d" % (k, t))
                     nc.scalar.activation(from_b[:], b_rows[t][:].indirect(b_list[:, part]), ACT.Copy)
                     nc.vector.tensor_tensor(totals[k][:, t, :], a_rows[t][:].indirect(a_list[:, part]), from_b[:], ALU.add)
-            sums = [total[:].rearrange("p t (m u) -> p m t u", u=PACK) for total in totals]
-            ms = slice(h * P // 2, (h + 1) * P // 2)
-            nc.vector.tensor_tensor(z_grouped[:, :, ms, :].rearrange("p u m t -> p m t u"), sums[0], sums[1], ALU.max)
+            sums.append(totals)
+            if h == 0:
+                for u in range(PACK):
+                    larger(0, u)
 
         z2_grouped = keep.tile([P, H, PACK], BF16, name="z2_grouped", align_bytes=64)
         z2_codes = keep.tile([P, H], U32, name="z2_codes", tag="wa_codes", align_bytes=64)
@@ -151,17 +169,21 @@ def tile_picked_momtpathbgate_none_p_kernel(tc, x_words, x_scales, wa, wb, gt, g
         for cols, copy in zip(halves, (nc.scalar.copy, nc.vector.tensor_copy)):
             interleave(copy, z2_grouped[:, cols, :], z2_planes[:, :, cols])
 
-        out_rows = out.rearrange("(m u) n -> u m n", u=PACK)
+        out_rows = out.rearrange("(g u i) n -> u g i n", u=PACK, i=4)
         for u in range(PACK):
             z_codes = keep.tile([P, P], U32, name="z_codes%d" % u, align_bytes=64)
             z_scales = keep.tile([P, P], U8, name="z_scales%d" % u, align_bytes=64)
-            quantize(z_codes[:], z_scales[:], z_grouped[:, u, :, :].rearrange("p m t -> p (m t)"))
+            larger(1, u)
             if u == 0:
                 quantize(z2_codes[:], z2_scales[:], z2_grouped[:].rearrange("p c t -> p (c t)"))
+            quantize(z_codes[:], z_scales[:], z_grouped[u][:].rearrange("p m t -> p (m t)"))
             bank = psum.tile([P, H], F32, name="cv_bank%d" % u, tag="right%d" % u)
             product(bank[:], z_codes[:], z_scales[:], z2_codes[:], z2_scales[:])
             cv = keep.tile([P, H], F32, name="cv%d" % u)
-            nc.vector.tensor_scalar(cv[:], bank[:], 0.0625, None, ALU.mult)
+            if u == 0:
+                nc.scalar.activation(cv[:], bank[:], ACT.Copy, scale=0.0625)
+            else:
+                nc.vector.tensor_scalar(cv[:], bank[:], 0.0625, None, ALU.mult)
             gate = keep.tile([P, H], F32, name="gate%d" % u)
             result = keep.tile([P, H], F32, name="result%d" % u)
             for h in range(2):
@@ -169,4 +191,4 @@ def tile_picked_momtpathbgate_none_p_kernel(tc, x_words, x_scales, wa, wb, gt, g
                 nc.scalar.activation(gate[:, halves[h]], cv[:].indirect(n5_l[:, part]), ACT.Sigmoid)
             for cols in (halves if u == PACK - 1 else [slice(0, H)]):
                 nc.vector.tensor_tensor(result[:, cols], cv[:, cols], gate[:, cols], ALU.mult)
-                nc.sync.dma_start(out_rows[u][:, cols], result[:, cols])
+                nc.sync.dma_start(out_rows[u][:, :, cols], result[:, cols])

@@ -39,15 +39,14 @@ def tile_picked_momtpathbgate_none_p_kernel(tc, x_words, x_scales, wa, wb, gt, g
             return raw
 
         halves = [slice(h * HALF, (h + 1) * HALF) for h in range(2)]
-        scale_rows = keep.tile([P, T // 4], I32, name="scale_rows", align_bytes=64)
         scale_table = keep.tile([P, T], U8, name="scale_table", align_bytes=64)
         word_table = keep.tile([P, T], I32, name="word_table", align_bytes=64)
         nc.vector.memset(scale_table[:].bitcast(I32), 0)
-
-        for q in range(4):
-            nc.sync.dma_start(scale_rows[32 * q:32 * q + 4, :], x_scales[0, 4 * q:4 * q + 4, :].bitcast(I32))
         two_l = load_list("two_l", two)
         offs_l = load_list("offs_l", offs)
+        n3_l = load_list("n3_l", n3)
+        for q in range(4):
+            nc.sync.dma_start(scale_table[32 * q:32 * q + 4, :].bitcast(I32), x_scales[0, 4 * q:4 * q + 4, :].bitcast(I32))
         nc.sync.dma_start(word_table[:], x_words[0].rearrange("p c r -> p (c r)").bitcast(I32))
         wb_raw = [load_weight("wb_raw%d" % h, wb, halves[h])[:] for h in range(2)]
         gains_by_tile = keep.tile([P, P], F32, name="gains_by_tile")
@@ -59,14 +58,12 @@ def tile_picked_momtpathbgate_none_p_kernel(tc, x_words, x_scales, wa, wb, gt, g
         for n, gain in enumerate((gt, gi)):
             nc.sync.dma_start(gains_by_tile[PACK * n:PACK * (n + 1), :].rearrange("t (g i) -> t g i", i=4),
                               gain.rearrange("(g t i) o -> t g (i o)", t=PACK, i=4))
-        n3_l = load_list("n3_l", n3)
         n4_l = load_list("n4_l", n4)
-        wa_raw = [load_weight("wa_raw%d" % h, wa, halves[h])[:] for h in range(2)]
+        wa_parts = [slice(0, 256), slice(256, 384), slice(384, 512)]
+        wa_raw = [load_weight("wa_raw%d" % n, wa, cols)[:] for n, cols in enumerate(wa_parts)]
         n1_l = load_list("n1_l", n1)
         n2_l = load_list("n2_l", n2)
         n5_l = load_list("n5_l", n5)
-        for q in range(4):
-            nc.vector.tensor_copy(scale_table[32 * q:32 * q + 4, :].bitcast(I32), scale_rows[32 * q:32 * q + 4, :])
 
         gains_bank = psum.tile([P, P], F32, name="gains_bank", tag="right3")
         nc.tensor.transpose(gains_bank[:], gains_by_tile[:], identity[:])
@@ -75,10 +72,10 @@ def tile_picked_momtpathbgate_none_p_kernel(tc, x_words, x_scales, wa, wb, gt, g
         gt_t, gi_t = gains[:, 0:PACK], gains[:, PACK:2 * PACK]
         gt_sign = keep.tile([P, PACK], F32, name="gt_sign")
         gt_step = keep.tile([P, PACK], F32, name="gt_step")
-        gi_signed = keep.tile([P, PACK], F32, name="gi_signed")
+        gi_signed = keep.tile([P, 1], F32, name="gi_signed")
         nc.gpsimd.tensor_scalar(gt_step[:], gt_t, 0.0, 2.0, ALU.is_ge, ALU.mult)
         nc.gpsimd.tensor_scalar(gt_sign[:], gt_step[:], 1.0, -1.0, ALU.mult, ALU.add)
-        nc.gpsimd.tensor_tensor(gi_signed[:], gi_t, gt_sign[:], ALU.mult)
+        nc.gpsimd.tensor_tensor(gi_signed[:], gi_t[:, 0:1], gt_sign[:, 0:1], ALU.mult)
 
         def pick_scales(name, lst):
             picked = keep.tile([P, S], U8, name=name + "_picked", align_bytes=64)
@@ -99,13 +96,13 @@ def tile_picked_momtpathbgate_none_p_kernel(tc, x_words, x_scales, wa, wb, gt, g
         def quantize(codes, scales, grouped):
             nc.vector.quantize_mx(out=codes.bitcast(FP8X4), scales=scales, in_=grouped)
 
-        def quantize_weight(name, raws, copies):
+        def quantize_weight(name, parts, raws, copies):
             codes = keep.tile([P, H], U32, name=name + "_codes", align_bytes=64)
             scales = keep.tile([P, H], U8, name=name + "_scales", align_bytes=64)
             grouped = keep.tile([P, H, PACK], BF16, name=name + "_grouped", align_bytes=64)
-            for h in range(2):
-                interleave(copies[h], grouped[:, halves[h], :], raws[h])
-            for cols in halves:
+            for cols, raw, copy in zip(parts, raws, copies):
+                interleave(copy, grouped[:, cols, :], raw)
+            for cols in parts:
                 quantize(codes[:, cols], scales[:, cols], grouped[:, cols, :].rearrange("p c t -> p (c t)"))
             return codes, scales
 
@@ -114,11 +111,11 @@ def tile_picked_momtpathbgate_none_p_kernel(tc, x_words, x_scales, wa, wb, gt, g
                                 rhs=rhs_codes.bitcast(FP8X4), rhs_scale=rhs_scales, start=True, stop=True)
 
         xb_scales = pick_scales("xb_scales", two_l)
-        xb_words = pick_words("xb_words", two_l)
-        wb_codes, wb_scales = quantize_weight("wb", wb_raw, [nc.scalar.copy, nc.scalar.copy])
         xa_scales = pick_scales("xa_scales", offs_l)
+        xb_words = pick_words("xb_words", two_l)
         xa_words = pick_words("xa_words", offs_l)
-        wa_codes, wa_scales = quantize_weight("wa", wa_raw, [nc.scalar.copy, nc.vector.tensor_copy])
+        wb_codes, wb_scales = quantize_weight("wb", halves, wb_raw, [nc.scalar.copy, nc.vector.tensor_copy])
+        wa_codes, wa_scales = quantize_weight("wa", wa_parts, wa_raw, [nc.scalar.copy, nc.vector.tensor_copy, nc.vector.tensor_copy])
         gt_abs = keep.tile([P, PACK], F32, name="gt_abs", tag="wa_raw0")
         nc.scalar.activation(gt_abs[:], gt_t, ACT.Abs)
 
@@ -130,65 +127,80 @@ def tile_picked_momtpathbgate_none_p_kernel(tc, x_words, x_scales, wa, wb, gt, g
             bank = psum.tile([P, H], F32, name="a_bank%d" % t, tag="right%d" % t)
             product(bank[:], xa_words[:, t, :], xa_scales[:, t, :], wa_codes[:], wa_scales[:])
             a_banks.append(bank)
-        a_rows = [keep.tile([P, H], F32, name="a_rows%d" % t) for t in range(PACK)]
-        b_rows = [keep.tile([P, H], F32, name="b_rows%d" % t, align_bytes=64) for t in range(PACK)]
+        a_rows = [keep.tile([P, 2 * H], F32, name="a_rows%d" % t, align_bytes=64) for t in range(PACK)]
+        b_rows = [keep.tile([P, 2 * H], F32, name="b_rows%d" % t, align_bytes=64) for t in range(PACK)]
 
-        z_grouped = [keep.tile([P, P, PACK], BF16, name="z_grouped%d" % u, align_bytes=64) for u in range(PACK)]
-        sums = []
+        def on_vector(dst, bank, factor):
+            nc.vector.tensor_scalar(dst, bank, factor, None, ALU.mult)
 
-        def larger(h, u):
-            first, second = [total[:].rearrange("p t (g u i) -> p u g t i", u=PACK, i=4)[:, u] for total in sums[h]]
-            dst = z_grouped[u][:, h * P // 2:(h + 1) * P // 2, :].rearrange("p (g i) t -> p g t i", i=4)
-            nc.vector.tensor_tensor(dst, first, second, ALU.max)
+        def on_scalar(dst, bank, factor):
+            nc.scalar.activation(dst, bank, ACT.Copy, scale=factor)
 
-        for h in range(2):
-            part = slice(h * LIST_COLS // 2, (h + 1) * LIST_COLS // 2)
-            totals = [keep.tile([P, PACK, HALF], F32, name="sum%d_%d" % (h, k)) for k in range(2)]
-            for t in range(PACK):
-                if h == 0:
-                    nc.scalar.activation(b_rows[t][:], b_banks[t][:], ACT.Copy, scale=gt_abs[:, t:t + 1])
-                    if t < 3:
-                        nc.vector.tensor_scalar(a_rows[t][:], a_banks[t][:], gt_abs[:, t:t + 1], None, ALU.mult)
-                    else:
-                        nc.scalar.activation(a_rows[t][:], a_banks[t][:], ACT.Copy, scale=gt_abs[:, t:t + 1])
-                for k, (a_list, b_list) in enumerate(((n1_l, n3_l), (n2_l, n4_l))):
-                    from_b = keep.tile([P, HALF], F32, name="from_b%d_%d" % (k, t))
-                    nc.scalar.activation(from_b[:], b_rows[t][:].indirect(b_list[:, part]), ACT.Copy)
-                    nc.vector.tensor_tensor(totals[k][:, t, :], a_rows[t][:].indirect(a_list[:, part]), from_b[:], ALU.add)
-            sums.append(totals)
-            if h == 0:
-                for u in range(PACK):
-                    larger(0, u)
+        z2_planes = keep.tile([P, PACK, H], BF16, name="z2_planes", tag="wa_raw2")
+        on_vector(z2_planes[:, 0, :], b_banks[0][:], gi_signed[:])
+        totals = [keep.tile([P, PACK, H], F32, name="sum%d" % k) for k in range(2)]
+        on_vector(a_rows[0][:, 0:H], a_banks[0][:], gt_abs[:, 0:1])
+        for t in range(PACK):
+            on_scalar(b_rows[t][:, 0:H], b_banks[t][:], gt_abs[:, t:t + 1])
+            for k, (a_list, b_list) in enumerate(((n1_l, n3_l), (n2_l, n4_l))):
+                from_b = keep.tile([P, H], F32, name="from_b%d_%d" % (k, 1 if t == 3 else t))
+                nc.scalar.activation(from_b[:], b_rows[t][:].indirect(b_list[:]), ACT.Copy)
+                nc.vector.tensor_tensor(totals[k][:, t, :], a_rows[t][:].indirect(a_list[:]), from_b[:], ALU.add)
+                if k == 0 and t + 1 < PACK:
+                    (on_scalar if t + 1 == 3 else on_vector)(a_rows[t + 1][:, 0:H], a_banks[t + 1][:], gt_abs[:, t + 1:t + 2])
 
-        z2_grouped = keep.tile([P, H, PACK], BF16, name="z2_grouped", align_bytes=64)
+        gi_later = keep.tile([P, PACK - 1], F32, name="gi_later", tag="from_b0_2")
+        nc.gpsimd.tensor_tensor(gi_later[:], gi_t[:, 1:PACK], gt_sign[:, 1:PACK], ALU.mult)
+        for t in range(1, PACK):
+            on_scalar(z2_planes[:, t, :], b_banks[t][:], gi_later[:, t - 1:t])
+
+        z2_grouped = keep.tile([P, H, PACK], BF16, name="z2_grouped", tag="a_rows2", align_bytes=64)
         z2_codes = keep.tile([P, H], U32, name="z2_codes", tag="wa_codes", align_bytes=64)
         z2_scales = keep.tile([P, H], U8, name="z2_scales", tag="wa_scales", align_bytes=64)
-        z2_planes = keep.tile([P, PACK, H], BF16, name="z2_planes", tag="b_rows3", align_bytes=64)
-        for t in range(PACK):
-            nc.scalar.activation(z2_planes[:, t, :], b_banks[t][:], ACT.Copy, scale=gi_signed[:, t:t + 1])
+
+        z_grouped = [keep.tile([P, P, PACK], BF16, name="z_grouped%d" % u, align_bytes=64) for u in range(PACK)]
+        z_codes = [keep.tile([P, P], U32, name="z_codes%d" % u, align_bytes=64) for u in range(PACK)]
+        z_scales = [keep.tile([P, P], U8, name="z_scales%d" % u, align_bytes=64) for u in range(PACK)]
+
+        def larger(u):
+            first, second = [total[:].rearrange("p t (g u i) -> p u g t i", u=PACK, i=4)[:, u] for total in totals]
+            nc.vector.tensor_tensor(z_grouped[u][:].rearrange("p (g i) t -> p g t i", i=4), first, second, ALU.max)
+
+        def quantize_z(u):
+            quantize(z_codes[u][:], z_scales[u][:], z_grouped[u][:].rearrange("p m t -> p (m t)"))
+
+        larger(0)
         for cols, copy in zip(halves, (nc.scalar.copy, nc.vector.tensor_copy)):
             interleave(copy, z2_grouped[:, cols, :], z2_planes[:, :, cols])
+        quantize_z(0)
+        quantize(z2_codes[:], z2_scales[:], z2_grouped[:].rearrange("p c t -> p (c t)"))
 
         out_rows = out.rearrange("(g u i) n -> u g i n", u=PACK, i=4)
-        for u in range(PACK):
-            z_codes = keep.tile([P, P], U32, name="z_codes%d" % u, align_bytes=64)
-            z_scales = keep.tile([P, P], U8, name="z_scales%d" % u, align_bytes=64)
-            larger(1, u)
-            if u == 0:
-                quantize(z2_codes[:], z2_scales[:], z2_grouped[:].rearrange("p c t -> p (c t)"))
-            quantize(z_codes[:], z_scales[:], z_grouped[u][:].rearrange("p m t -> p (m t)"))
+        cv_rows = [keep.tile([P, 2 * H], F32, name="cv_rows%d" % u) for u in range(PACK)]
+
+        def moments(u):
             bank = psum.tile([P, H], F32, name="cv_bank%d" % u, tag="right%d" % u)
-            product(bank[:], z_codes[:], z_scales[:], z2_codes[:], z2_scales[:])
-            cv = keep.tile([P, H], F32, name="cv%d" % u)
-            if u == 0:
-                nc.scalar.activation(cv[:], bank[:], ACT.Copy, scale=0.0625)
-            else:
-                nc.vector.tensor_scalar(cv[:], bank[:], 0.0625, None, ALU.mult)
+            product(bank[:], z_codes[u][:], z_scales[u][:], z2_codes[:], z2_scales[:])
+            (on_scalar if u < 2 else on_vector)(cv_rows[u][:, 0:H], bank[:], 0.0625)
+
+        def finish(u):
             gate = keep.tile([P, H], F32, name="gate%d" % u)
             result = keep.tile([P, H], F32, name="result%d" % u)
-            for h in range(2):
-                part = slice(h * LIST_COLS // 2, (h + 1) * LIST_COLS // 2)
-                nc.scalar.activation(gate[:, halves[h]], cv[:].indirect(n5_l[:, part]), ACT.Sigmoid)
             for cols in (halves if u == PACK - 1 else [slice(0, H)]):
-                nc.vector.tensor_tensor(result[:, cols], cv[:, cols], gate[:, cols], ALU.mult)
+                part = slice(cols.start // 16, cols.stop // 16)
+                nc.scalar.activation(gate[:, cols], cv_rows[u][:].indirect(n5_l[:, part]), ACT.Sigmoid)
+                nc.vector.tensor_tensor(result[:, cols], cv_rows[u][:, cols], gate[:, cols], ALU.mult)
                 nc.sync.dma_start(out_rows[u][:, :, cols], result[:, cols])
+
+        moments(0)
+        larger(1)
+        larger(2)
+        quantize_z(1)
+        larger(3)
+        quantize_z(2)
+        quantize_z(3)
+        finish(0)
+        for u in range(1, PACK):
+            moments(u)
+        for u in range(1, PACK):
+            finish(u)

@@ -1,7 +1,7 @@
 from contextlib import ExitStack
 
 import concourse.mybir as mybir
-from concourse.masks import make_identity
+from concourse.masks import make_block_diagonal, make_identity
 
 K, T, S, H = 512, 2048, 512, 512
 FLOPS = 3 * 2 * 512 * 512 * 512
@@ -44,38 +44,32 @@ def tile_picked_momtpathbgate_none_p_kernel(tc, x_words, x_scales, wa, wb, gt, g
         nc.vector.memset(scale_table[:].bitcast(I32), 0)
         two_l = load_list("two_l", two)
         offs_l = load_list("offs_l", offs)
-        n3_l = load_list("n3_l", n3)
+        loaded = [keep.tile([P, PACK], F32, name="gain%d" % n) for n in range(2)]
+        nc.sync.dma_start(loaded[0][:], gt.rearrange("(p i) o -> p (i o)", i=4))
         for q in range(4):
             nc.sync.dma_start(scale_table[32 * q:32 * q + 4, :].bitcast(I32), x_scales[0, 4 * q:4 * q + 4, :].bitcast(I32))
         nc.sync.dma_start(word_table[:], x_words[0].rearrange("p c r -> p (c r)").bitcast(I32))
+        nc.sync.dma_start(loaded[1][:], gi.rearrange("(p i) o -> p (i o)", i=4))
         wb_raw = [load_weight("wb_raw%d" % h, wb, halves[h])[:] for h in range(2)]
-        gains_by_tile = keep.tile([P, P], F32, name="gains_by_tile")
-        identity = keep.tile([P, P], F32, name="identity")
-        nc.gpsimd.memset(gains_by_tile[:], 0.0)
-        make_identity(nc, identity[:])
-        unread = keep.tile([P, 1], F32, name="unread")
-        nc.scalar.activation(unread[:], identity[:, 0:1], ACT.Sigmoid)
-        for n, gain in enumerate((gt, gi)):
-            nc.sync.dma_start(gains_by_tile[PACK * n:PACK * (n + 1), :].rearrange("t (g i) -> t g i", i=4),
-                              gain.rearrange("(g t i) o -> t g (i o)", t=PACK, i=4))
+        n3_l = load_list("n3_l", n3)
+        wa_raw = [load_weight("wa_raw%d" % h, wa, halves[h])[:] for h in range(2)]
         n4_l = load_list("n4_l", n4)
-        wa_parts = [slice(0, 256), slice(256, 384), slice(384, 512)]
-        wa_raw = [load_weight("wa_raw%d" % n, wa, cols)[:] for n, cols in enumerate(wa_parts)]
         n1_l = load_list("n1_l", n1)
         n2_l = load_list("n2_l", n2)
         n5_l = load_list("n5_l", n5)
 
-        gains_bank = psum.tile([P, P], F32, name="gains_bank", tag="right3")
-        nc.tensor.transpose(gains_bank[:], gains_by_tile[:], identity[:])
-        gains = keep.tile([P, 2 * PACK], F32, name="gains")
-        nc.scalar.copy(gains[:], gains_bank[:, 0:2 * PACK])
-        gt_t, gi_t = gains[:, 0:PACK], gains[:, PACK:2 * PACK]
-        gt_sign = keep.tile([P, PACK], F32, name="gt_sign")
-        gt_step = keep.tile([P, PACK], F32, name="gt_step")
-        gi_signed = keep.tile([P, 1], F32, name="gi_signed")
-        nc.gpsimd.tensor_scalar(gt_step[:], gt_t, 0.0, 2.0, ALU.is_ge, ALU.mult)
-        nc.gpsimd.tensor_scalar(gt_sign[:], gt_step[:], 1.0, -1.0, ALU.mult, ALU.add)
-        nc.gpsimd.tensor_tensor(gi_signed[:], gi_t[:, 0:1], gt_sign[:, 0:1], ALU.mult)
+        gains_bank = psum.tile([P, 2, P], F32, name="gains_bank", tag="right3")
+        identity = keep.tile([P, P], F32, name="identity")
+        same_group = keep.tile([P, P], F32, name="same_group")
+        make_identity(nc, identity[:])
+        make_block_diagonal(nc, same_group[:], 4)
+        unread = keep.tile([P, 1], F32, name="unread")
+        nc.scalar.activation(unread[:], identity[:, 0:1], ACT.Sigmoid)
+        for n, gain in enumerate(loaded):
+            spread = keep.tile([P, P // 4, 4], F32, name="spread%d" % n)
+            nc.gpsimd.tensor_tensor(spread[:], same_group[:].rearrange("p (g i) -> p g i", i=4),
+                                    gain[:].unsqueeze(1).to_broadcast([P, P // 4, 4]), ALU.mult)
+            nc.tensor.transpose(gains_bank[:, n, :], spread[:].rearrange("p g i -> p (g i)"), identity[:])
 
         def pick_scales(name, lst):
             picked = keep.tile([P, S], U8, name=name + "_picked", align_bytes=64)
@@ -115,7 +109,18 @@ def tile_picked_momtpathbgate_none_p_kernel(tc, x_words, x_scales, wa, wb, gt, g
         xb_words = pick_words("xb_words", two_l)
         xa_words = pick_words("xa_words", offs_l)
         wb_codes, wb_scales = quantize_weight("wb", halves, wb_raw, [nc.scalar.copy, nc.vector.tensor_copy])
-        wa_codes, wa_scales = quantize_weight("wa", wa_parts, wa_raw, [nc.scalar.copy, nc.vector.tensor_copy, nc.vector.tensor_copy])
+        gains = keep.tile([P, 2 * PACK], F32, name="gains", tag="wb_raw0")
+        nc.vector.tensor_reduce(gains[:].rearrange("p (n t) -> p n t", n=2),
+                                gains_bank[:].rearrange("p n (g t) -> p n t g", t=PACK), mybir.AxisListType.X, ALU.add)
+        gt_t, gi_t = gains[:, 0:PACK], gains[:, PACK:2 * PACK]
+        gt_sign = keep.tile([P, PACK], F32, name="gt_sign")
+        gt_step = keep.tile([P, PACK], F32, name="gt_step")
+        gi_signed = keep.tile([P, 1], F32, name="gi_signed")
+        nc.gpsimd.tensor_scalar(gt_step[:], gt_t, 0.0, 2.0, ALU.is_ge, ALU.mult)
+        nc.gpsimd.tensor_scalar(gt_sign[:], gt_step[:], 1.0, -1.0, ALU.mult, ALU.add)
+        nc.gpsimd.tensor_tensor(gi_signed[:], gi_t[:, 0:1], gt_sign[:, 0:1], ALU.mult)
+
+        wa_codes, wa_scales = quantize_weight("wa", halves, wa_raw, [nc.scalar.copy, nc.vector.tensor_copy])
         gt_abs = keep.tile([P, PACK], F32, name="gt_abs", tag="wa_raw0")
         nc.scalar.activation(gt_abs[:], gt_t, ACT.Abs)
 
@@ -136,7 +141,7 @@ def tile_picked_momtpathbgate_none_p_kernel(tc, x_words, x_scales, wa, wb, gt, g
         def on_scalar(dst, bank, factor):
             nc.scalar.activation(dst, bank, ACT.Copy, scale=factor)
 
-        z2_planes = keep.tile([P, PACK, H], BF16, name="z2_planes", tag="wa_raw2")
+        z2_planes = keep.tile([P, PACK, H], BF16, name="z2_planes", tag="wa_raw1")
         on_vector(z2_planes[:, 0, :], b_banks[0][:], gi_signed[:])
         totals = [keep.tile([P, PACK, H], F32, name="sum%d" % k) for k in range(2)]
         on_vector(a_rows[0][:, 0:H], a_banks[0][:], gt_abs[:, 0:1])

@@ -90,13 +90,13 @@ def tile_picked_momtpathbgate_none_p_kernel(tc, x_words, x_scales, wa, wb, gt, g
         def quantize(codes, scales, grouped):
             nc.vector.quantize_mx(out=codes.bitcast(FP8X4), scales=scales, in_=grouped)
 
-        def quantize_weight(name, parts, raws, copies):
+        def quantize_weight(name, parts, raws, copies, calls):
             codes = keep.tile([P, H], U32, name=name + "_codes", align_bytes=64)
             scales = keep.tile([P, H], U8, name=name + "_scales", align_bytes=64)
             grouped = keep.tile([P, H, PACK], BF16, name=name + "_grouped", align_bytes=64)
             for cols, raw, copy in zip(parts, raws, copies):
                 interleave(copy, grouped[:, cols, :], raw)
-            for cols in parts:
+            for cols in calls:
                 quantize(codes[:, cols], scales[:, cols], grouped[:, cols, :].rearrange("p c t -> p (c t)"))
             return codes, scales
 
@@ -108,7 +108,7 @@ def tile_picked_momtpathbgate_none_p_kernel(tc, x_words, x_scales, wa, wb, gt, g
         xa_scales = pick_scales("xa_scales", offs_l)
         xb_words = pick_words("xb_words", two_l)
         xa_words = pick_words("xa_words", offs_l)
-        wb_codes, wb_scales = quantize_weight("wb", halves, wb_raw, [nc.scalar.copy, nc.vector.tensor_copy])
+        wb_codes, wb_scales = quantize_weight("wb", halves, wb_raw, [nc.scalar.copy, nc.vector.tensor_copy], halves)
         gains = keep.tile([P, 2 * PACK], F32, name="gains", tag="wb_raw0")
         nc.vector.tensor_reduce(gains[:].rearrange("p (n t) -> p n t", n=2),
                                 gains_bank[:].rearrange("p n (g t) -> p n t g", t=PACK), mybir.AxisListType.X, ALU.add)
@@ -120,7 +120,7 @@ def tile_picked_momtpathbgate_none_p_kernel(tc, x_words, x_scales, wa, wb, gt, g
         nc.gpsimd.tensor_scalar(gt_sign[:], gt_step[:], 1.0, -1.0, ALU.mult, ALU.add)
         nc.gpsimd.tensor_tensor(gi_signed[:], gi_t[:, 0:1], gt_sign[:, 0:1], ALU.mult)
 
-        wa_codes, wa_scales = quantize_weight("wa", halves, wa_raw, [nc.scalar.copy, nc.vector.tensor_copy])
+        wa_codes, wa_scales = quantize_weight("wa", halves, wa_raw, [nc.scalar.copy, nc.vector.tensor_copy], [slice(0, H)])
         gt_abs = keep.tile([P, PACK], F32, name="gt_abs", tag="wa_raw0")
         nc.scalar.activation(gt_abs[:], gt_t, ACT.Abs)
 
@@ -141,7 +141,7 @@ def tile_picked_momtpathbgate_none_p_kernel(tc, x_words, x_scales, wa, wb, gt, g
         def on_scalar(dst, bank, factor):
             nc.scalar.activation(dst, bank, ACT.Copy, scale=factor)
 
-        z2_planes = keep.tile([P, PACK, H], BF16, name="z2_planes", tag="wa_raw1")
+        z2_planes = keep.tile([P, PACK, H], BF16, name="z2_planes", tag="wa_grouped", align_bytes=64)
         on_vector(z2_planes[:, 0, :], b_banks[0][:], gi_signed[:])
         totals = [keep.tile([P, PACK, H], F32, name="sum%d" % k) for k in range(2)]
         on_vector(a_rows[0][:, 0:H], a_banks[0][:], gt_abs[:, 0:1])

from contextlib import ExitStack

import concourse.mybir as mybir
from concourse.masks import make_block_diagonal, make_identity

K, T, S, H = 512, 2048, 512, 512
FLOPS = 3 * 2 * 512 * 512 * 512

F32 = mybir.dt.float32
BF16 = mybir.dt.bfloat16
I32 = mybir.dt.int32
U32 = mybir.dt.uint32
U16 = mybir.dt.uint16
U8 = mybir.dt.uint8
FP8X4 = mybir.dt.float8_e4m3fn_x4
ALU = mybir.AluOpType
ACT = mybir.ActivationFunctionType

P = 128
PACK = 4
HALF = H // 2
LIST_COLS = S // 16


def tile_picked_momtpathbgate_none_p_kernel(tc, x_words, x_scales, wa, wb, gt, gi, offs, two, n1, n2, n3, n4, n5, out):
    nc = tc.nc
    with ExitStack() as ctx:
        keep = ctx.enter_context(tc.tile_pool(name="keep", bufs=1))
        psum = ctx.enter_context(tc.psum_pool(name="psum", bufs=1))

        def load_list(name, src):
            lst = keep.tile([P, LIST_COLS], U16, name=name)
            nc.sync.dma_start(lst[:], src)
            return lst

        def load_weight(name, w, cols):
            raw = keep.tile([P, PACK, cols.stop - cols.start], F32, name=name)
            nc.sync.dma_start(raw[:], w.rearrange("(p j) n -> p j n", j=PACK)[:, :, cols])
            return raw

        halves = [slice(h * HALF, (h + 1) * HALF) for h in range(2)]
        scale_table = keep.tile([P, T], U8, name="scale_table", align_bytes=64)
        word_table = keep.tile([P, T], I32, name="word_table", align_bytes=64)
        nc.vector.memset(scale_table[:].bitcast(I32), 0)
        two_l = load_list("two_l", two)
        offs_l = load_list("offs_l", offs)
        loaded = [keep.tile([P, PACK], F32, name="gain%d" % n) for n in range(2)]
        nc.sync.dma_start(loaded[0][:], gt.rearrange("(p i) o -> p (i o)", i=4))
        for q in range(4):
            nc.sync.dma_start(scale_table[32 * q:32 * q + 4, :].bitcast(I32), x_scales[0, 4 * q:4 * q + 4, :].bitcast(I32))
        nc.sync.dma_start(word_table[:], x_words[0].rearrange("p c r -> p (c r)").bitcast(I32))
        nc.sync.dma_start(loaded[1][:], gi.rearrange("(p i) o -> p (i o)", i=4))
        wb_raw = [load_weight("wb_raw%d" % h, wb, halves[h])[:] for h in range(2)]
        n3_l = load_list("n3_l", n3)
        wa_raw = [load_weight("wa_raw%d" % h, wa, halves[h])[:] for h in range(2)]
        n4_l = load_list("n4_l", n4)
        n1_l = load_list("n1_l", n1)
        n2_l = load_list("n2_l", n2)
        n5_l = load_list("n5_l", n5)

        gains_bank = psum.tile([P, 2, P], F32, name="gains_bank", tag="right3")
        identity = keep.tile([P, P], F32, name="identity")
        same_group = keep.tile([P, P], F32, name="same_group")
        make_identity(nc, identity[:])
        make_block_diagonal(nc, same_group[:], 4)
        unread = keep.tile([P, 1], F32, name="unread")
        nc.scalar.activation(unread[:], identity[:, 0:1], ACT.Sigmoid)
        for n, gain in enumerate(loaded):
            spread = keep.tile([P, P // 4, 4], F32, name="spread%d" % n)
            nc.gpsimd.tensor_tensor(spread[:], same_group[:].rearrange("p (g i) -> p g i", i=4),
                                    gain[:].unsqueeze(1).to_broadcast([P, P // 4, 4]), ALU.mult)
            nc.tensor.transpose(gains_bank[:, n, :], spread[:].rearrange("p g i -> p (g i)"), identity[:])

        def pick_scales(name, lst):
            picked = keep.tile([P, S], U8, name=name + "_picked", align_bytes=64)
            dealt = keep.tile([P, S], U8, name=name + "_dealt", align_bytes=64)
            nc.vector.tensor_copy(picked[:], scale_table[:].indirect(lst[:]))
            nc.vector.tensor_copy(dealt[:].bitcast(I32).rearrange("p (t g) -> p t g", t=PACK),
                                  picked[:].bitcast(I32).rearrange("p (g t) -> p t g", t=PACK))
            return dealt[:].rearrange("p (t m) -> p t m", t=PACK)

        def pick_words(name, lst):
            dealt = keep.tile([P, PACK, P], U32, name=name, align_bytes=64)
            nc.vector.tensor_copy(dealt[:].rearrange("p t (g i) -> p g t i", i=4), word_table[:].bitcast(U32).indirect(lst[:]))
            return dealt

        def interleave(copy, dst, src):
            copy(dst.rearrange("p (c i) t -> p c t i", i=4), src.rearrange("p t (c i) -> p c t i", i=4))

        def quantize(codes, scales, grouped):
            nc.vector.quantize_mx(out=codes.bitcast(FP8X4), scales=scales, in_=grouped)

        def quantize_weight(name, parts, raws, copies, calls):
            codes = keep.tile([P, H], U32, name=name + "_codes", align_bytes=64)
            scales = keep.tile([P, H], U8, name=name + "_scales", align_bytes=64)
            grouped = keep.tile([P, H, PACK], BF16, name=name + "_grouped", align_bytes=64)
            for cols, raw, copy in zip(parts, raws, copies):
                interleave(copy, grouped[:, cols, :], raw)
            for cols in calls:
                quantize(codes[:, cols], scales[:, cols], grouped[:, cols, :].rearrange("p c t -> p (c t)"))
            return codes, scales

        def product(bank, lhs_codes, lhs_scales, rhs_codes, rhs_scales):
            nc.tensor.matmul_mx(out=bank, lhsT=lhs_codes.bitcast(FP8X4), lhsT_scale=lhs_scales,
                                rhs=rhs_codes.bitcast(FP8X4), rhs_scale=rhs_scales, start=True, stop=True)

        xb_scales = pick_scales("xb_scales", two_l)
        xa_scales = pick_scales("xa_scales", offs_l)
        xb_words = pick_words("xb_words", two_l)
        xa_words = pick_words("xa_words", offs_l)
        wb_codes, wb_scales = quantize_weight("wb", halves, wb_raw, [nc.scalar.copy, nc.vector.tensor_copy], halves)
        gains = keep.tile([P, 2 * PACK], F32, name="gains", tag="wb_raw0")
        nc.vector.tensor_reduce(gains[:].rearrange("p (n t) -> p n t", n=2),
                                gains_bank[:].rearrange("p n (g t) -> p n t g", t=PACK), mybir.AxisListType.X, ALU.add)
        gt_t, gi_t = gains[:, 0:PACK], gains[:, PACK:2 * PACK]
        gt_sign = keep.tile([P, PACK], F32, name="gt_sign")
        gt_step = keep.tile([P, PACK], F32, name="gt_step")
        gi_signed = keep.tile([P, 1], F32, name="gi_signed")
        nc.gpsimd.tensor_scalar(gt_step[:], gt_t, 0.0, 2.0, ALU.is_ge, ALU.mult)
        nc.gpsimd.tensor_scalar(gt_sign[:], gt_step[:], 1.0, -1.0, ALU.mult, ALU.add)
        nc.gpsimd.tensor_tensor(gi_signed[:], gi_t[:, 0:1], gt_sign[:, 0:1], ALU.mult)

        wa_codes, wa_scales = quantize_weight("wa", halves, wa_raw, [nc.scalar.copy, nc.vector.tensor_copy], [slice(0, H)])
        gt_abs = keep.tile([P, PACK], F32, name="gt_abs", tag="wa_raw0")
        nc.scalar.activation(gt_abs[:], gt_t, ACT.Abs)

        b_banks, a_banks = [], []
        for t in range(PACK):
            bank = psum.tile([P, H], F32, name="b_bank%d" % t, tag="left%d" % t)
            product(bank[:], xb_words[:, t, :], xb_scales[:, t, :], wb_codes[:], wb_scales[:])
            b_banks.append(bank)
            bank = psum.tile([P, H], F32, name="a_bank%d" % t, tag="right%d" % t)
            product(bank[:], xa_words[:, t, :], xa_scales[:, t, :], wa_codes[:], wa_scales[:])
            a_banks.append(bank)
        a_rows = [keep.tile([P, 2 * H], F32, name="a_rows%d" % t, align_bytes=64) for t in range(PACK)]
        b_rows = [keep.tile([P, 2 * H], F32, name="b_rows%d" % t, align_bytes=64) for t in range(PACK)]

        def on_vector(dst, bank, factor):
            nc.vector.tensor_scalar(dst, bank, factor, None, ALU.mult)

        def on_scalar(dst, bank, factor):
            nc.scalar.activation(dst, bank, ACT.Copy, scale=factor)

        z2_planes = keep.tile([P, PACK, H], BF16, name="z2_planes", tag="wa_grouped", align_bytes=64)
        on_vector(z2_planes[:, 0, :], b_banks[0][:], gi_signed[:])
        totals = [keep.tile([P, PACK, H], F32, name="sum%d" % k) for k in range(2)]
        on_vector(a_rows[0][:, 0:H], a_banks[0][:], gt_abs[:, 0:1])
        for t in range(PACK):
            on_scalar(b_rows[t][:, 0:H], b_banks[t][:], gt_abs[:, t:t + 1])
            for k, (a_list, b_list) in enumerate(((n1_l, n3_l), (n2_l, n4_l))):
                from_b = keep.tile([P, H], F32, name="from_b%d_%d" % (k, 1 if t == 3 else t))
                nc.scalar.activation(from_b[:], b_rows[t][:].indirect(b_list[:]), ACT.Copy)
                nc.vector.tensor_tensor(totals[k][:, t, :], a_rows[t][:].indirect(a_list[:]), from_b[:], ALU.add)
                if k == 0 and t + 1 < PACK:
                    (on_scalar if t + 1 == 3 else on_vector)(a_rows[t + 1][:, 0:H], a_banks[t + 1][:], gt_abs[:, t + 1:t + 2])

        gi_later = keep.tile([P, PACK - 1], F32, name="gi_later", tag="from_b0_2")
        nc.gpsimd.tensor_tensor(gi_later[:], gi_t[:, 1:PACK], gt_sign[:, 1:PACK], ALU.mult)
        for t in range(1, PACK):
            on_scalar(z2_planes[:, t, :], b_banks[t][:], gi_later[:, t - 1:t])

        z2_grouped = keep.tile([P, H, PACK], BF16, name="z2_grouped", tag="a_rows2", align_bytes=64)
        z2_codes = keep.tile([P, H], U32, name="z2_codes", tag="wa_codes", align_bytes=64)
        z2_scales = keep.tile([P, H], U8, name="z2_scales", tag="wa_scales", align_bytes=64)

        z_grouped = [keep.tile([P, P, PACK], BF16, name="z_grouped%d" % u, align_bytes=64) for u in range(PACK)]
        z_codes = [keep.tile([P, P], U32, name="z_codes%d" % u, align_bytes=64) for u in range(PACK)]
        z_scales = [keep.tile([P, P], U8, name="z_scales%d" % u, align_bytes=64) for u in range(PACK)]

        def larger(u):
            first, second = [total[:].rearrange("p t (g u i) -> p u g t i", u=PACK, i=4)[:, u] for total in totals]
            nc.vector.tensor_tensor(z_grouped[u][:].rearrange("p (g i) t -> p g t i", i=4), first, second, ALU.max)

        def quantize_z(u):
            quantize(z_codes[u][:], z_scales[u][:], z_grouped[u][:].rearrange("p m t -> p (m t)"))

        larger(0)
        for cols, copy in zip(halves, (nc.scalar.copy, nc.vector.tensor_copy)):
            interleave(copy, z2_grouped[:, cols, :], z2_planes[:, :, cols])
        quantize_z(0)
        quantize(z2_codes[:], z2_scales[:], z2_grouped[:].rearrange("p c t -> p (c t)"))

        out_rows = out.rearrange("(g u i) n -> u g i n", u=PACK, i=4)
        cv_rows = [keep.tile([P, 2 * H], F32, name="cv_rows%d" % u) for u in range(PACK)]

        def moments(u):
            bank = psum.tile([P, H], F32, name="cv_bank%d" % u, tag="right%d" % u)
            product(bank[:], z_codes[u][:], z_scales[u][:], z2_codes[:], z2_scales[:])
            (on_scalar if u < 2 else on_vector)(cv_rows[u][:, 0:H], bank[:], 0.0625)

        def finish(u):
            gate = keep.tile([P, H], F32, name="gate%d" % u)
            result = keep.tile([P, H], F32, name="result%d" % u)
            for cols in (halves if u == PACK - 1 else [slice(0, H)]):
                part = slice(cols.start // 16, cols.stop // 16)
                nc.scalar.activation(gate[:, cols], cv_rows[u][:].indirect(n5_l[:, part]), ACT.Sigmoid)
                nc.vector.tensor_tensor(result[:, cols], cv_rows[u][:, cols], gate[:, cols], ALU.mult)
                nc.sync.dma_start(out_rows[u][:, :, cols], result[:, cols])

        moments(0)
        larger(1)
        larger(2)
        quantize_z(1)
        larger(3)
        quantize_z(2)
        quantize_z(3)
        finish(0)
        for u in range(1, PACK):
            moments(u)
        for u in range(1, PACK):
            finish(u)
